import numpy as np
import ml_dtypes


def mxq(x, axis, fmt="e4m3"):
    dtype, down = {"e4m3": (ml_dtypes.float8_e4m3fn, 7), "e5m2": (ml_dtypes.float8_e5m2, 14)}[fmt]
    v = np.moveaxis(np.asarray(x, np.float32).astype(ml_dtypes.bfloat16).astype(np.float64), axis, -1)
    blocks = v.reshape(v.shape[:-1] + (-1, 32))
    amax = np.abs(blocks).max(-1, keepdims=True)
    byte = np.maximum(np.where(amax > 0, np.frexp(amax)[1] - 1 + 127, 0) - down, 1)
    scale = np.exp2(byte - 127.0)
    codes = (blocks / scale).astype(np.float32).astype(dtype).astype(np.float64)
    return np.moveaxis((codes * scale).reshape(v.shape), -1, axis)


WIDE = False


def mx_kscale(k):
    if not WIDE:
        return np.ones(k)
    levels = np.array([10, -10, 5, -5, 0])
    if k % 512:
        return np.exp2(np.random.permutation(np.resize(levels, k // 32))).repeat(32)
    a = np.empty((k // 512, 16))
    for p in range(k // 512):
        a[p, :8] = np.random.permutation(np.resize(levels, 8))
        for g in range(8):
            far = levels[np.abs(levels - a[p, g]) >= 10]
            a[p, g + 8] = far[np.random.randint(len(far))]
    return np.exp2(a.ravel()).repeat(32)


def f64(x):
    return np.asarray(x).astype(np.float64)


def striped(idx):
    return np.tile(idx.reshape(-1, 16).T, (8, 1)).astype(np.uint16)


def unstriped(offs):
    return offs[:16].T.reshape(-1).astype(np.int64)


def pack_weight(w):
    k, n = w.shape
    w = f64(np.asarray(w, np.float32).astype(ml_dtypes.bfloat16)).reshape(k // 32, 32, n)
    amax = np.abs(w).max(1)
    byte = np.clip(np.where(amax > 0, np.frexp(amax)[1] - 1 + 127 - 7, 1), 1, 254)
    scaled = (w * np.exp2(127.0 - byte)[:, None, :]).reshape(k, n).astype(np.float32)
    words = np.ascontiguousarray(scaled.reshape(k // 512, 128, 4, n).transpose(0, 1, 3, 2)).astype(ml_dtypes.float8_e4m3fn).view(np.uint8)
    return words, np.ascontiguousarray(byte.astype(np.uint8).reshape(k // 512, 16, n))


def unpack_weight(words, scales):
    g, p, n, _ = words.shape
    vals = np.ascontiguousarray(words).view(ml_dtypes.float8_e4m3fn).astype(np.float64) * np.repeat(np.exp2(scales.astype(np.float64) - 127.0), 8, axis=1)[..., None]
    return vals.transpose(0, 1, 3, 2).reshape(g * 512, n)


def planes(y):
    n, m = y.shape
    v = y.astype(np.float32).astype(ml_dtypes.bfloat16).astype(np.float64).reshape(n // 32, 32, m)
    top = np.abs(v).max(1)
    byte = np.clip(np.where(top > 0, np.frexp(top)[1] - 1 + 127 - 7, 1), 1, 254)
    codes = (v * np.exp2(127.0 - byte)[:, None, :]).reshape(n, m).astype(np.float32).astype(ml_dtypes.float8_e4m3fn).view(np.uint8)
    words = codes.reshape(n // 512, 128, 4, m).transpose(0, 1, 3, 2)
    return np.ascontiguousarray(words), np.ascontiguousarray(byte.astype(np.uint8).reshape(n // 512, 16, m))


def relu(v):
    return np.maximum(v, 0.0)


K, T, S, W, H, N = 1024, 2048, 512, 1024, 512, 512


def setup_inputs():
    n = np.random.standard_normal
    s = mx_kscale(K)[:, None]
    u = mx_kscale(H)
    packed_xT = pack_weight(n((K, T)) * s)
    packed_eT = pack_weight(n((K, W)) * s)
    packed_w3 = pack_weight(n((H, N)) / np.sqrt(H) / u[:, None])
    return {
        "x_words": packed_xT[0],
        "x_scales": packed_xT[1],
        "e_words": packed_eT[0],
        "e_scales": packed_eT[1],
        "w1": (n((K, H)) / np.sqrt(2 * K) / s * u).astype(np.float32),
        "w2": (n((K, H)) / np.sqrt(2 * K) / s * u).astype(np.float32),
        "w3_words": packed_w3[0],
        "w3_scales": packed_w3[1],
        "skip": (n((N, S))).astype(np.float32),
        "offs": striped(np.random.permutation(T)[:S]),
        "tok": striped(np.random.permutation(W)[:S]),
    }


def reference(x_words, x_scales, e_words, e_scales, w1, w2, w3_words, w3_scales, skip, offs, tok):
    xq = unpack_weight(x_words, x_scales)[:, unstriped(offs)]
    e_tok = unpack_weight(e_words, e_scales)[:, unstriped(tok)]
    h = relu(mxq(f64(w1), 0, "e4m3").T @ xq + mxq(f64(w2), 0, "e4m3").T @ e_tok)
    y = unpack_weight(w3_words, w3_scales).T @ mxq(h, 0, "e4m3")
    out_0 = y + f64(skip)
    return (out_0,) + planes(out_0)

@@ -1,0 +1,198 @@
+from contextlib import ExitStack
+
+import concourse.mybir as mybir
+
+K, T, S, W, H, N = 1024, 2048, 512, 1024, 512, 512
+FLOPS = 2 * S * (2 * K * H + H * N)
+
+F32 = mybir.dt.float32
+BF16 = mybir.dt.bfloat16
+I32 = mybir.dt.int32
+U32 = mybir.dt.uint32
+U16 = mybir.dt.uint16
+U8 = mybir.dt.uint8
+FP8X4 = mybir.dt.float8_e4m3fn_x4
+ACT = mybir.ActivationFunctionType
+ADD = mybir.AluOpType.add
+
+P = 128
+PACK = 4
+K_PASS = P * PACK
+PASSES = K // K_PASS
+QUADS = 4
+QUAD = 32
+CHUNK = 128
+CHUNKS = S // CHUNK
+LIST_ROWS = 16
+X_ROW, E_ROW, W3_ROW = 0, 8, 8
+ALIGN = 64
+
+
+def tile_picked_zeagle_relu_po_kernel(
+    tc, x_words, x_scales, e_words, e_scales, w1, w2, w3_words, w3_scales, skip, offs, tok, out_0, out_1, out_2
+):
+    nc = tc.nc
+    with ExitStack() as ctx:
+        keep = ctx.enter_context(tc.tile_pool(name="keep", bufs=1))
+        psum = ctx.enter_context(tc.psum_pool(name="psum", bufs=1))
+
+        def words_view(dram, g):
+            return dram[g].rearrange("p n t -> p (n t)").bitcast(I32)
+
+        def cleared(width, name):
+            tile = keep.tile([P, width], U8, name=name, align_bytes=ALIGN)
+            nc.vector.memset(tile[:].bitcast(I32), 0)
+            return tile
+
+        def load_scales(queue, tile, dram, row):
+            passes = dram.shape[0]
+            for q in range(QUADS):
+                first = QUAD * q + row
+                queue.dma_start(
+                    out=tile[first : first + PACK * passes, :].bitcast(I32),
+                    in_=dram[:, PACK * q : PACK * (q + 1), :].bitcast(I32),
+                )
+
+        e_sc = cleared(W, "e_sc")
+        x_sc = cleared(T, "x_sc")
+        w3_sc = cleared(N, "w3_sc")
+        load_scales(nc.gpsimd, x_sc, x_scales, X_ROW)
+        load_scales(nc.gpsimd, w3_sc, w3_scales, W3_ROW)
+
+        weights = [(w2, 0), (w2, 1), (w1, 0), (w1, 1)]
+        w_raw = []
+        tok_list = keep.tile([P, S // LIST_ROWS], U16, name="tok_list")
+        offs_list = keep.tile([P, S // LIST_ROWS], U16, name="offs_list")
+        for i, (w, g) in enumerate(weights):
+            raw = keep.tile([P, PACK, H], F32, name="w_raw%d" % i, tag="raw%d" % i, align_bytes=ALIGN)
+            nc.sync.dma_start(out=raw[:], in_=w[g * K_PASS : (g + 1) * K_PASS, :].rearrange("(p j) c -> p j c", j=PACK))
+            w_raw.append(raw)
+            if i == 0:
+                nc.sync.dma_start(tok_list[:], tok)
+                nc.sync.dma_start(offs_list[:], offs)
+            if i == 1:
+                load_scales(nc.sync, e_sc, e_scales, E_ROW)
+        w_codes, w_sc = [], []
+        for i, raw in enumerate(w_raw):
+            grouped = keep.tile([P, PACK * H], BF16, name="w_grouped%d" % i, tag="grouped%d" % i, align_bytes=ALIGN)
+            dst = grouped[:].rearrange("p (t m j) -> p m t j", t=PACK, j=PACK)
+            src = raw[:].rearrange("p j (m t) -> p m t j", t=PACK)
+            if i == 1:
+                nc.vector.tensor_copy(out=dst, in_=src)
+            else:
+                nc.scalar.activation(out=dst, in_=src, func=ACT.Copy)
+            codes = keep.tile([P, H], U32, name="w_codes%d" % i, align_bytes=ALIGN)
+            scales = keep.tile([P, H], U8, name="w_sc%d" % i, align_bytes=ALIGN)
+            nc.vector.quantize_mx(out=codes[:].bitcast(FP8X4), scales=scales[:], in_=grouped[:])
+            w_codes.append(codes)
+            w_sc.append(scales)
+
+        tables = []
+        for i, (dram, g, width, tag) in enumerate(
+            [(e_words, 0, W, "raw0"), (e_words, 1, W, "grouped0"), (x_words, 0, T, "raw1"), (x_words, 1, T, "raw2")]
+        ):
+            table = keep.tile([P, width], U32, name="table%d" % i, tag=tag, align_bytes=ALIGN)
+            nc.sync.dma_start(out=table[:].bitcast(I32), in_=words_view(dram, g))
+            tables.append(table)
+        w3_raw = keep.tile([P, N], I32, name="w3_raw", tag="grouped2", align_bytes=ALIGN)
+        nc.sync.dma_start(out=w3_raw[:], in_=words_view(w3_words, 0))
+        skip_rows = skip.rearrange("(p t) n -> p t n", t=PACK)
+        skip_half = []
+        for u in range(2):
+            half = keep.tile([P, PACK, S // 2], F32, name="skip%d" % u, tag=("raw3", "grouped3")[u], align_bytes=ALIGN)
+            nc.sync.dma_start(out=half[:], in_=skip_rows[:, :, u * (S // 2) : (u + 1) * (S // 2)])
+            skip_half.append(half)
+
+        e_sc_picked = keep.tile([P, S], U8, name="e_sc_picked", align_bytes=ALIGN)
+        nc.vector.tensor_copy(e_sc_picked[:], e_sc[:].indirect(tok_list[:]))
+        x_sc_picked = keep.tile([P, S], U8, name="x_sc_picked", tag="grouped1", align_bytes=ALIGN)
+        nc.vector.tensor_copy(x_sc_picked[:], x_sc[:].indirect(offs_list[:]))
+
+        hidden = [psum.tile([P, PACK, CHUNK], F32, name="hidden%d" % c) for c in range(CHUNKS)]
+        sources = [
+            (tables[0], tok_list, e_sc_picked, E_ROW, S),
+            (tables[1], tok_list, e_sc_picked, E_ROW + PACK, S),
+            (tables[2], offs_list, x_sc_picked, X_ROW, S // 2),
+            (tables[3], offs_list, x_sc_picked, X_ROW + PACK, CHUNK),
+        ]
+        last = len(sources) - 1
+        for i, (table, picks, picked_sc, row, width) in enumerate(sources):
+            for s0 in range(0, S, width):
+                picked = keep.tile([P, width], U32, name="picked%d_%d" % (i, s0), align_bytes=ALIGN)
+                nc.vector.tensor_copy(
+                    picked[:], table[:].indirect(picks[:, s0 // LIST_ROWS : (s0 + width) // LIST_ROWS])
+                )
+                for c0 in range(0, width, CHUNK):
+                    c = (s0 + c0) // CHUNK
+                    for t in range(PACK):
+                        cols = slice(t * P, (t + 1) * P)
+                        nc.tensor.matmul_mx(
+                            out=hidden[c][:, t, :],
+                            lhsT=w_codes[i][:, cols].bitcast(FP8X4),
+                            lhsT_scale=w_sc[i][:, cols],
+                            rhs=picked[:, c0 : c0 + CHUNK].bitcast(FP8X4),
+                            rhs_scale=picked_sc[row:P, c * CHUNK : (c + 1) * CHUNK],
+                            start=(i == 0 and t == 0),
+                            stop=(i == last and t == PACK - 1),
+                        )
+
+        w3_sc_dealt = keep.tile([P, N], U8, name="w3_sc_dealt", tag="raw1", align_bytes=ALIGN)
+        nc.vector.tensor_copy(
+            out=w3_sc_dealt[:].rearrange("p (t m) -> p t m", t=PACK),
+            in_=w3_sc[:].rearrange("p (m t) -> p t m", t=PACK),
+        )
+        w3_dealt = keep.tile([P, N], I32, name="w3_dealt", align_bytes=ALIGN)
+        nc.vector.tensor_copy(
+            out=w3_dealt[:].rearrange("p (t a b) -> p a t b", t=PACK, b=PACK),
+            in_=w3_raw[:].rearrange("p (a b t) -> p a t b", t=PACK, b=PACK),
+        )
+
+        out_rows = out_0.rearrange("(p t) n -> p t n", t=PACK)
+        out_words = words_view(out_1, 0)
+        y_sc = keep.tile([P, S], U8, name="y_sc", align_bytes=ALIGN)
+        result = []
+        for c in range(CHUNKS):
+            h_bf = keep.tile([P, CHUNK, PACK], BF16, name="h_bf%d" % c, align_bytes=ALIGN)
+            nc.scalar.activation(out=h_bf[:], in_=hidden[c][:].rearrange("p t n -> p n t"), func=ACT.Relu)
+            h_codes = keep.tile([P, CHUNK], U32, name="h_codes%d" % c, align_bytes=ALIGN)
+            h_sc = keep.tile([P, CHUNK], U8, name="h_sc%d" % c, align_bytes=ALIGN)
+            nc.vector.quantize_mx(
+                out=h_codes[:].bitcast(FP8X4), scales=h_sc[:], in_=h_bf[:].rearrange("p n t -> p (n t)")
+            )
+            bank = psum.tile([P, PACK, CHUNK], F32, name="result%d" % c)
+            for t in range(PACK):
+                cols = slice(t * P, (t + 1) * P)
+                nc.tensor.matmul_mx(
+                    out=bank[:, t, :],
+                    lhsT=w3_dealt[:, cols].bitcast(FP8X4),
+                    lhsT_scale=w3_sc_dealt[W3_ROW:P, cols],
+                    rhs=h_codes[:].bitcast(FP8X4),
+                    rhs_scale=h_sc[:],
+                    start=True,
+                    stop=True,
+                )
+            result.append(bank)
+
+        for c in range(CHUNKS):
+            cols = slice(c * CHUNK, (c + 1) * CHUNK)
+            u, c0 = divmod(c * CHUNK, S // 2)
+            y = keep.tile([P, PACK, CHUNK], F32, name="y%d" % c, align_bytes=ALIGN)
+            nc.vector.tensor_tensor(out=y[:], in0=result[c][:], in1=skip_half[u][:, :, c0 : c0 + CHUNK], op=ADD)
+            nc.sync.dma_start(out=out_rows[:, :, cols], in_=y[:])
+            y_bf = keep.tile([P, CHUNK, PACK], BF16, name="y_bf%d" % c, align_bytes=ALIGN)
+            nc.scalar.activation(
+                out=y_bf[:].rearrange("p (a b) t -> p a t b", b=PACK),
+                in_=y[:].rearrange("p t (a b) -> p a t b", b=PACK),
+                func=ACT.Copy,
+            )
+            y_codes = keep.tile([P, CHUNK], U32, name="y_codes%d" % c, align_bytes=ALIGN)
+            nc.vector.quantize_mx(
+                out=y_codes[:].bitcast(FP8X4), scales=y_sc[:, cols], in_=y_bf[:].rearrange("p n t -> p (n t)")
+            )
+            nc.sync.dma_start(out=out_words[:, cols], in_=y_codes[:].bitcast(I32))
+        for q in range(QUADS):
+            queue = nc.scalar if q % 2 else nc.sync
+            queue.dma_start(
+                out=out_2[0, PACK * q : PACK * (q + 1), :].bitcast(I32),
+                in_=y_sc[QUAD * q : QUAD * q + PACK, :].bitcast(I32),
+            )

@@ -39,9 +39,9 @@ def tile_picked_zeagle_relu_po_kernel(
         def words_view(dram, g):
             return dram[g].rearrange("p n t -> p (n t)").bitcast(I32)
 
-        def cleared(width, name):
+        def cleared(engine, width, name):
             tile = keep.tile([P, width], U8, name=name, align_bytes=ALIGN)
-            nc.vector.memset(tile[:].bitcast(I32), 0)
+            engine.memset(tile[:].bitcast(I32), 0)
             return tile
 
         def load_scales(queue, tile, dram, row):
@@ -53,25 +53,27 @@ def tile_picked_zeagle_relu_po_kernel(
                     in_=dram[:, PACK * q : PACK * (q + 1), :].bitcast(I32),
                 )
 
-        e_sc = cleared(W, "e_sc")
-        x_sc = cleared(T, "x_sc")
-        w3_sc = cleared(N, "w3_sc")
-        load_scales(nc.gpsimd, x_sc, x_scales, X_ROW)
-        load_scales(nc.gpsimd, w3_sc, w3_scales, W3_ROW)
+        e_sc = cleared(nc.gpsimd, W, "e_sc")
+        x_sc = cleared(nc.vector, T, "x_sc")
+        w3_sc = cleared(nc.vector, N, "w3_sc")
 
         weights = [(w2, 0), (w2, 1), (w1, 0), (w1, 1)]
         w_raw = []
         tok_list = keep.tile([P, S // LIST_ROWS], U16, name="tok_list")
         offs_list = keep.tile([P, S // LIST_ROWS], U16, name="offs_list")
+        nc.sync.dma_start(tok_list[:], tok)
+        nc.sync.dma_start(offs_list[:], offs)
         for i, (w, g) in enumerate(weights):
-            raw = keep.tile([P, PACK, H], F32, name="w_raw%d" % i, tag="raw%d" % i, align_bytes=ALIGN)
+            raw = keep.tile([P, PACK, H], F32, name="w_raw%d" % i, align_bytes=ALIGN)
             nc.sync.dma_start(out=raw[:], in_=w[g * K_PASS : (g + 1) * K_PASS, :].rearrange("(p j) c -> p j c", j=PACK))
             w_raw.append(raw)
             if i == 0:
-                nc.sync.dma_start(tok_list[:], tok)
-                nc.sync.dma_start(offs_list[:], offs)
-            if i == 1:
                 load_scales(nc.sync, e_sc, e_scales, E_ROW)
+            if i == 2:
+                load_scales(nc.sync, x_sc, x_scales, X_ROW)
+        e_sc_picked = keep.tile([P, S], U8, name="e_sc_picked", align_bytes=ALIGN)
+        nc.vector.tensor_copy(e_sc_picked[:], e_sc[:].indirect(tok_list[:]))
+
         w_codes, w_sc = [], []
         for i, raw in enumerate(w_raw):
             grouped = keep.tile([P, PACK * H], BF16, name="w_grouped%d" % i, tag="grouped%d" % i, align_bytes=ALIGN)
@@ -88,23 +90,21 @@ def tile_picked_zeagle_relu_po_kernel(
             w_sc.append(scales)
 
         tables = []
-        for i, (dram, g, width, tag) in enumerate(
-            [(e_words, 0, W, "raw0"), (e_words, 1, W, "grouped0"), (x_words, 0, T, "raw1"), (x_words, 1, T, "raw2")]
-        ):
-            table = keep.tile([P, width], U32, name="table%d" % i, tag=tag, align_bytes=ALIGN)
+        for i, (dram, g, width) in enumerate([(e_words, 0, W), (e_words, 1, W), (x_words, 0, T), (x_words, 1, T)]):
+            table = keep.tile([P, width], U32, name="table%d" % i, tag="table%d" % i, align_bytes=ALIGN)
             nc.sync.dma_start(out=table[:].bitcast(I32), in_=words_view(dram, g))
             tables.append(table)
-        w3_raw = keep.tile([P, N], I32, name="w3_raw", tag="grouped2", align_bytes=ALIGN)
+            if i == 2:
+                load_scales(nc.sync, w3_sc, w3_scales, W3_ROW)
+        w3_raw = keep.tile([P, N], I32, name="w3_raw", align_bytes=ALIGN)
         nc.sync.dma_start(out=w3_raw[:], in_=words_view(w3_words, 0))
         skip_rows = skip.rearrange("(p t) n -> p t n", t=PACK)
         skip_half = []
         for u in range(2):
-            half = keep.tile([P, PACK, S // 2], F32, name="skip%d" % u, tag=("raw3", "grouped3")[u], align_bytes=ALIGN)
+            half = keep.tile([P, PACK, S // 2], F32, name="skip%d" % u, align_bytes=ALIGN)
             nc.sync.dma_start(out=half[:], in_=skip_rows[:, :, u * (S // 2) : (u + 1) * (S // 2)])
             skip_half.append(half)
 
-        e_sc_picked = keep.tile([P, S], U8, name="e_sc_picked", align_bytes=ALIGN)
-        nc.vector.tensor_copy(e_sc_picked[:], e_sc[:].indirect(tok_list[:]))
         x_sc_picked = keep.tile([P, S], U8, name="x_sc_picked", tag="grouped1", align_bytes=ALIGN)
         nc.vector.tensor_copy(x_sc_picked[:], x_sc[:].indirect(offs_list[:]))
 
@@ -136,7 +136,7 @@ def tile_picked_zeagle_relu_po_kernel(
                             stop=(i == last and t == PACK - 1),
                         )
 
-        w3_sc_dealt = keep.tile([P, N], U8, name="w3_sc_dealt", tag="raw1", align_bytes=ALIGN)
+        w3_sc_dealt = keep.tile([P, N], U8, name="w3_sc_dealt", tag="table2", align_bytes=ALIGN)
         nc.vector.tensor_copy(
             out=w3_sc_dealt[:].rearrange("p (t m) -> p t m", t=PACK),
             in_=w3_sc[:].rearrange("p (m t) -> p t m", t=PACK),
@@ -180,11 +180,12 @@ def tile_picked_zeagle_relu_po_kernel(
             nc.vector.tensor_tensor(out=y[:], in0=result[c][:], in1=skip_half[u][:, :, c0 : c0 + CHUNK], op=ADD)
             nc.sync.dma_start(out=out_rows[:, :, cols], in_=y[:])
             y_bf = keep.tile([P, CHUNK, PACK], BF16, name="y_bf%d" % c, align_bytes=ALIGN)
-            nc.scalar.activation(
-                out=y_bf[:].rearrange("p (a b) t -> p a t b", b=PACK),
-                in_=y[:].rearrange("p t (a b) -> p a t b", b=PACK),
-                func=ACT.Copy,
-            )
+            dst = y_bf[:].rearrange("p (a b) t -> p a t b", b=PACK)
+            src = y[:].rearrange("p t (a b) -> p a t b", b=PACK)
+            if c == CHUNKS - 1:
+                nc.vector.tensor_copy(out=dst, in_=src)
+            else:
+                nc.scalar.activation(out=dst, in_=src, func=ACT.Copy)
             y_codes = keep.tile([P, CHUNK], U32, name="y_codes%d" % c, align_bytes=ALIGN)
             nc.vector.quantize_mx(
                 out=y_codes[:].bitcast(FP8X4), scales=y_sc[:, cols], in_=y_bf[:].rearrange("p n t -> p (n t)")

@@ -24,7 +24,7 @@ QUAD = 32
 CHUNK = 128
 CHUNKS = S // CHUNK
 LIST_ROWS = 16
-X_ROW, E_ROW, W3_ROW = 0, 8, 8
+X_ROW, E_ROW, W3_ROW = 8, 0, 0
 ALIGN = 64
 
 
@@ -56,21 +56,20 @@ def tile_picked_zeagle_relu_po_kernel(
         e_sc = cleared(nc.gpsimd, W, "e_sc")
         x_sc = cleared(nc.vector, T, "x_sc")
         w3_sc = cleared(nc.vector, N, "w3_sc")
+        load_scales(nc.gpsimd, x_sc, x_scales, X_ROW)
 
         weights = [(w2, 0), (w2, 1), (w1, 0), (w1, 1)]
         w_raw = []
         tok_list = keep.tile([P, S // LIST_ROWS], U16, name="tok_list")
         offs_list = keep.tile([P, S // LIST_ROWS], U16, name="offs_list")
-        nc.sync.dma_start(tok_list[:], tok)
-        nc.sync.dma_start(offs_list[:], offs)
         for i, (w, g) in enumerate(weights):
             raw = keep.tile([P, PACK, H], F32, name="w_raw%d" % i, align_bytes=ALIGN)
             nc.sync.dma_start(out=raw[:], in_=w[g * K_PASS : (g + 1) * K_PASS, :].rearrange("(p j) c -> p j c", j=PACK))
             w_raw.append(raw)
             if i == 0:
+                nc.sync.dma_start(tok_list[:], tok)
+                nc.sync.dma_start(offs_list[:], offs)
                 load_scales(nc.sync, e_sc, e_scales, E_ROW)
-            if i == 2:
-                load_scales(nc.sync, x_sc, x_scales, X_ROW)
         e_sc_picked = keep.tile([P, S], U8, name="e_sc_picked", align_bytes=ALIGN)
         nc.vector.tensor_copy(e_sc_picked[:], e_sc[:].indirect(tok_list[:]))
 
@@ -79,7 +78,7 @@ def tile_picked_zeagle_relu_po_kernel(
             grouped = keep.tile([P, PACK * H], BF16, name="w_grouped%d" % i, tag="grouped%d" % i, align_bytes=ALIGN)
             dst = grouped[:].rearrange("p (t m j) -> p m t j", t=PACK, j=PACK)
             src = raw[:].rearrange("p j (m t) -> p m t j", t=PACK)
-            if i == 1:
+            if i == 2:
                 nc.vector.tensor_copy(out=dst, in_=src)
             else:
                 nc.scalar.activation(out=dst, in_=src, func=ACT.Copy)
@@ -105,7 +104,7 @@ def tile_picked_zeagle_relu_po_kernel(
             nc.sync.dma_start(out=half[:], in_=skip_rows[:, :, u * (S // 2) : (u + 1) * (S // 2)])
             skip_half.append(half)
 
-        x_sc_picked = keep.tile([P, S], U8, name="x_sc_picked", tag="grouped1", align_bytes=ALIGN)
+        x_sc_picked = keep.tile([P, S], U8, name="x_sc_picked", tag="grouped0", align_bytes=ALIGN)
         nc.vector.tensor_copy(x_sc_picked[:], x_sc[:].indirect(offs_list[:]))
 
         hidden = [psum.tile([P, PACK, CHUNK], F32, name="hidden%d" % c) for c in range(CHUNKS)]

from contextlib import ExitStack

import concourse.mybir as mybir

K, T, S, W, H, N = 1024, 2048, 512, 1024, 512, 512
FLOPS = 2 * S * (2 * K * H + H * N)

F32 = mybir.dt.float32
BF16 = mybir.dt.bfloat16
I32 = mybir.dt.int32
U32 = mybir.dt.uint32
U16 = mybir.dt.uint16
U8 = mybir.dt.uint8
FP8X4 = mybir.dt.float8_e4m3fn_x4
ACT = mybir.ActivationFunctionType
ADD = mybir.AluOpType.add

P = 128
PACK = 4
K_PASS = P * PACK
PASSES = K // K_PASS
QUADS = 4
QUAD = 32
CHUNK = 128
CHUNKS = S // CHUNK
LIST_ROWS = 16
X_ROW, E_ROW, W3_ROW = 8, 0, 0
ALIGN = 64


def tile_picked_zeagle_relu_po_kernel(
    tc, x_words, x_scales, e_words, e_scales, w1, w2, w3_words, w3_scales, skip, offs, tok, out_0, out_1, out_2
):
    nc = tc.nc
    with ExitStack() as ctx:
        keep = ctx.enter_context(tc.tile_pool(name="keep", bufs=1))
        psum = ctx.enter_context(tc.psum_pool(name="psum", bufs=1))

        def words_view(dram, g):
            return dram[g].rearrange("p n t -> p (n t)").bitcast(I32)

        def cleared(engine, width, name):
            tile = keep.tile([P, width], U8, name=name, align_bytes=ALIGN)
            engine.memset(tile[:].bitcast(I32), 0)
            return tile

        def load_scales(queue, tile, dram, row):
            passes = dram.shape[0]
            for q in range(QUADS):
                first = QUAD * q + row
                queue.dma_start(
                    out=tile[first : first + PACK * passes, :].bitcast(I32),
                    in_=dram[:, PACK * q : PACK * (q + 1), :].bitcast(I32),
                )

        e_sc = cleared(nc.gpsimd, W, "e_sc")
        x_sc = cleared(nc.vector, T, "x_sc")
        w3_sc = cleared(nc.vector, N, "w3_sc")
        load_scales(nc.gpsimd, x_sc, x_scales, X_ROW)

        weights = [(w2, 0), (w2, 1), (w1, 0), (w1, 1)]
        w_raw = []
        tok_list = keep.tile([P, S // LIST_ROWS], U16, name="tok_list")
        offs_list = keep.tile([P, S // LIST_ROWS], U16, name="offs_list")
        for i, (w, g) in enumerate(weights):
            raw = keep.tile([P, PACK, H], F32, name="w_raw%d" % i, align_bytes=ALIGN)
            nc.sync.dma_start(out=raw[:], in_=w[g * K_PASS : (g + 1) * K_PASS, :].rearrange("(p j) c -> p j c", j=PACK))
            w_raw.append(raw)
            if i == 0:
                nc.sync.dma_start(tok_list[:], tok)
                nc.sync.dma_start(offs_list[:], offs)
                load_scales(nc.sync, e_sc, e_scales, E_ROW)
        e_sc_picked = keep.tile([P, S], U8, name="e_sc_picked", align_bytes=ALIGN)
        nc.vector.tensor_copy(e_sc_picked[:], e_sc[:].indirect(tok_list[:]))

        w_codes, w_sc = [], []
        for i, raw in enumerate(w_raw):
            grouped = keep.tile([P, PACK * H], BF16, name="w_grouped%d" % i, tag="grouped%d" % i, align_bytes=ALIGN)
            dst = grouped[:].rearrange("p (t m j) -> p m t j", t=PACK, j=PACK)
            src = raw[:].rearrange("p j (m t) -> p m t j", t=PACK)
            if i == 2:
                nc.vector.tensor_copy(out=dst, in_=src)
            else:
                nc.scalar.activation(out=dst, in_=src, func=ACT.Copy)
            codes = keep.tile([P, H], U32, name="w_codes%d" % i, align_bytes=ALIGN)
            scales = keep.tile([P, H], U8, name="w_sc%d" % i, align_bytes=ALIGN)
            nc.vector.quantize_mx(out=codes[:].bitcast(FP8X4), scales=scales[:], in_=grouped[:])
            w_codes.append(codes)
            w_sc.append(scales)

        tables = []
        for i, (dram, g, width) in enumerate([(e_words, 0, W), (e_words, 1, W), (x_words, 0, T), (x_words, 1, T)]):
            table = keep.tile([P, width], U32, name="table%d" % i, tag="table%d" % i, align_bytes=ALIGN)
            nc.sync.dma_start(out=table[:].bitcast(I32), in_=words_view(dram, g))
            tables.append(table)
            if i == 2:
                load_scales(nc.sync, w3_sc, w3_scales, W3_ROW)
        w3_raw = keep.tile([P, N], I32, name="w3_raw", align_bytes=ALIGN)
        nc.sync.dma_start(out=w3_raw[:], in_=words_view(w3_words, 0))
        skip_rows = skip.rearrange("(p t) n -> p t n", t=PACK)
        skip_half = []
        for u in range(2):
            half = keep.tile([P, PACK, S // 2], F32, name="skip%d" % u, align_bytes=ALIGN)
            nc.sync.dma_start(out=half[:], in_=skip_rows[:, :, u * (S // 2) : (u + 1) * (S // 2)])
            skip_half.append(half)

        x_sc_picked = keep.tile([P, S], U8, name="x_sc_picked", tag="grouped0", align_bytes=ALIGN)
        nc.vector.tensor_copy(x_sc_picked[:], x_sc[:].indirect(offs_list[:]))

        hidden = [psum.tile([P, PACK, CHUNK], F32, name="hidden%d" % c) for c in range(CHUNKS)]
        sources = [
            (tables[0], tok_list, e_sc_picked, E_ROW, S),
            (tables[1], tok_list, e_sc_picked, E_ROW + PACK, S),
            (tables[2], offs_list, x_sc_picked, X_ROW, S // 2),
            (tables[3], offs_list, x_sc_picked, X_ROW + PACK, CHUNK),
        ]
        last = len(sources) - 1
        for i, (table, picks, picked_sc, row, width) in enumerate(sources):
            for s0 in range(0, S, width):
                picked = keep.tile([P, width], U32, name="picked%d_%d" % (i, s0), align_bytes=ALIGN)
                nc.vector.tensor_copy(
                    picked[:], table[:].indirect(picks[:, s0 // LIST_ROWS : (s0 + width) // LIST_ROWS])
                )
                for c0 in range(0, width, CHUNK):
                    c = (s0 + c0) // CHUNK
                    for t in range(PACK):
                        cols = slice(t * P, (t + 1) * P)
                        nc.tensor.matmul_mx(
                            out=hidden[c][:, t, :],
                            lhsT=w_codes[i][:, cols].bitcast(FP8X4),
                            lhsT_scale=w_sc[i][:, cols],
                            rhs=picked[:, c0 : c0 + CHUNK].bitcast(FP8X4),
                            rhs_scale=picked_sc[row:P, c * CHUNK : (c + 1) * CHUNK],
                            start=(i == 0 and t == 0),
                            stop=(i == last and t == PACK - 1),
                        )

        w3_sc_dealt = keep.tile([P, N], U8, name="w3_sc_dealt", tag="table2", align_bytes=ALIGN)
        nc.vector.tensor_copy(
            out=w3_sc_dealt[:].rearrange("p (t m) -> p t m", t=PACK),
            in_=w3_sc[:].rearrange("p (m t) -> p t m", t=PACK),
        )
        w3_dealt = keep.tile([P, N], I32, name="w3_dealt", align_bytes=ALIGN)
        nc.vector.tensor_copy(
            out=w3_dealt[:].rearrange("p (t a b) -> p a t b", t=PACK, b=PACK),
            in_=w3_raw[:].rearrange("p (a b t) -> p a t b", t=PACK, b=PACK),
        )

        out_rows = out_0.rearrange("(p t) n -> p t n", t=PACK)
        out_words = words_view(out_1, 0)
        y_sc = keep.tile([P, S], U8, name="y_sc", align_bytes=ALIGN)
        result = []
        for c in range(CHUNKS):
            h_bf = keep.tile([P, CHUNK, PACK], BF16, name="h_bf%d" % c, align_bytes=ALIGN)
            nc.scalar.activation(out=h_bf[:], in_=hidden[c][:].rearrange("p t n -> p n t"), func=ACT.Relu)
            h_codes = keep.tile([P, CHUNK], U32, name="h_codes%d" % c, align_bytes=ALIGN)
            h_sc = keep.tile([P, CHUNK], U8, name="h_sc%d" % c, align_bytes=ALIGN)
            nc.vector.quantize_mx(
                out=h_codes[:].bitcast(FP8X4), scales=h_sc[:], in_=h_bf[:].rearrange("p n t -> p (n t)")
            )
            bank = psum.tile([P, PACK, CHUNK], F32, name="result%d" % c)
            for t in range(PACK):
                cols = slice(t * P, (t + 1) * P)
                nc.tensor.matmul_mx(
                    out=bank[:, t, :],
                    lhsT=w3_dealt[:, cols].bitcast(FP8X4),
                    lhsT_scale=w3_sc_dealt[W3_ROW:P, cols],
                    rhs=h_codes[:].bitcast(FP8X4),
                    rhs_scale=h_sc[:],
                    start=True,
                    stop=True,
                )
            result.append(bank)

        for c in range(CHUNKS):
            cols = slice(c * CHUNK, (c + 1) * CHUNK)
            u, c0 = divmod(c * CHUNK, S // 2)
            y = keep.tile([P, PACK, CHUNK], F32, name="y%d" % c, align_bytes=ALIGN)
            nc.vector.tensor_tensor(out=y[:], in0=result[c][:], in1=skip_half[u][:, :, c0 : c0 + CHUNK], op=ADD)
            nc.sync.dma_start(out=out_rows[:, :, cols], in_=y[:])
            y_bf = keep.tile([P, CHUNK, PACK], BF16, name="y_bf%d" % c, align_bytes=ALIGN)
            dst = y_bf[:].rearrange("p (a b) t -> p a t b", b=PACK)
            src = y[:].rearrange("p t (a b) -> p a t b", b=PACK)
            if c == CHUNKS - 1:
                nc.vector.tensor_copy(out=dst, in_=src)
            else:
                nc.scalar.activation(out=dst, in_=src, func=ACT.Copy)
            y_codes = keep.tile([P, CHUNK], U32, name="y_codes%d" % c, align_bytes=ALIGN)
            nc.vector.quantize_mx(
                out=y_codes[:].bitcast(FP8X4), scales=y_sc[:, cols], in_=y_bf[:].rearrange("p n t -> p (n t)")
            )
            nc.sync.dma_start(out=out_words[:, cols], in_=y_codes[:].bitcast(I32))
        for q in range(QUADS):
            queue = nc.scalar if q % 2 else nc.sync
            queue.dma_start(
                out=out_2[0, PACK * q : PACK * (q + 1), :].bitcast(I32),
                in_=y_sc[QUAD * q : QUAD * q + PACK, :].bitcast(I32),
            )
